import numpy as np
import ml_dtypes


def mxq(x, axis, fmt="e4m3"):
    dtype, down = {"e4m3": (ml_dtypes.float8_e4m3fn, 7), "e5m2": (ml_dtypes.float8_e5m2, 14)}[fmt]
    v = np.moveaxis(np.asarray(x, np.float32).astype(ml_dtypes.bfloat16).astype(np.float64), axis, -1)
    blocks = v.reshape(v.shape[:-1] + (-1, 32))
    amax = np.abs(blocks).max(-1, keepdims=True)
    byte = np.maximum(np.where(amax > 0, np.frexp(amax)[1] - 1 + 127, 0) - down, 1)
    scale = np.exp2(byte - 127.0)
    codes = (blocks / scale).astype(np.float32).astype(dtype).astype(np.float64)
    return np.moveaxis((codes * scale).reshape(v.shape), -1, axis)


WIDE = False


def mx_kscale(k):
    if not WIDE:
        return np.ones(k)
    levels = np.array([10, -10, 5, -5, 0])
    if k % 512:
        return np.exp2(np.random.permutation(np.resize(levels, k // 32))).repeat(32)
    a = np.empty((k // 512, 16))
    for p in range(k // 512):
        a[p, :8] = np.random.permutation(np.resize(levels, 8))
        for g in range(8):
            far = levels[np.abs(levels - a[p, g]) >= 10]
            a[p, g + 8] = far[np.random.randint(len(far))]
    return np.exp2(a.ravel()).repeat(32)


def f64(x):
    return np.asarray(x).astype(np.float64)


def striped(idx):
    return np.tile(idx.reshape(-1, 16).T, (8, 1)).astype(np.uint16)


def unstriped(offs):
    return offs[:16].T.reshape(-1).astype(np.int64)


def striped8(idx):
    return np.concatenate([x.reshape(-1, 16).T for x in idx]).astype(np.uint16)


def runs(offs, k):
    lists = np.stack([offs[16 * r : 16 * r + 16].T.reshape(-1) for r in range(8)]).astype(np.int64)
    return lists[np.arange(k) % 512 // 64]


def pack_weight(w):
    k, n = w.shape
    w = f64(np.asarray(w, np.float32).astype(ml_dtypes.bfloat16)).reshape(k // 32, 32, n)
    amax = np.abs(w).max(1)
    byte = np.clip(np.where(amax > 0, np.frexp(amax)[1] - 1 + 127 - 7, 1), 1, 254)
    scaled = (w * np.exp2(127.0 - byte)[:, None, :]).reshape(k, n).astype(np.float32)
    words = np.ascontiguousarray(scaled.reshape(k // 512, 128, 4, n).transpose(0, 1, 3, 2)).astype(ml_dtypes.float8_e4m3fn).view(np.uint8)
    return words, np.ascontiguousarray(byte.astype(np.uint8).reshape(k // 512, 16, n))


def unpack_weight(words, scales):
    g, p, n, _ = words.shape
    vals = np.ascontiguousarray(words).view(ml_dtypes.float8_e4m3fn).astype(np.float64) * np.repeat(np.exp2(scales.astype(np.float64) - 127.0), 8, axis=1)[..., None]
    return vals.transpose(0, 1, 3, 2).reshape(g * 512, n)


def sigmoid(v):
    return 1.0 / (1.0 + np.exp(-np.maximum(v, -700.0)))

def planes(y):
    n, m = y.shape
    v = y.astype(np.float32).astype(ml_dtypes.bfloat16).astype(np.float64).reshape(n // 32, 32, m)
    top = np.abs(v).max(1)
    byte = np.clip(np.where(top > 0, np.frexp(top)[1] - 1 + 127 - 7, 1), 1, 254)
    codes = (v * np.exp2(127.0 - byte)[:, None, :]).reshape(n, m).astype(np.float32).astype(ml_dtypes.float8_e4m3fn).view(np.uint8)
    words = codes.reshape(n // 512, 128, 4, m).transpose(0, 1, 3, 2)
    return np.ascontiguousarray(words), np.ascontiguousarray(byte.astype(np.uint8).reshape(n // 512, 16, m))


K, T, S, G, H, U = 512, 1024, 256, 2048, 512, 512


def setup_inputs():
    n = np.random.standard_normal
    s = mx_kscale(K)[:, None]
    packed_xT = pack_weight(n((K, T)) * s)
    packed_dT = pack_weight(n((K, G)) / s)
    perm = np.random.permutation(U)
    return {
        "x_words": packed_xT[0],
        "x_scales": packed_xT[1],
        "d_words": packed_dT[0],
        "d_scales": packed_dT[1],
        "gs": (np.random.uniform(0.5, 1.5, (K, 1)) * s).astype(np.float32),
        "offs": striped8(np.random.randint(0, T, (8, S))),
        "ci": striped(np.random.permutation(G)[:H]),
        "n1": striped8(np.stack([np.random.permutation(S) for _ in range(8)])),
        "n2": striped8(np.stack([np.random.permutation(S) for _ in range(8)])),
        "k1": striped8(np.random.randint(0, G, (8, H))),
        "n3": striped(perm[:S]),
        "n4": striped(perm[S:]),
        "n5": striped(np.random.permutation(S)),
    }


def reference(x_words, x_scales, d_words, d_scales, gs, offs, ci, n1, n2, k1, n3, n4, n5):
    d_k1 = unpack_weight(d_words, d_scales)[np.arange(K)[:, None], runs(k1, K)]
    d_ci = unpack_weight(d_words, d_scales)[:, unstriped(ci)]
    xq = unpack_weight(x_words, x_scales)[np.arange(K)[:, None], runs(offs, K)]
    s = 0.0625 * (d_ci.T @ xq)
    st = s[np.arange(H)[:, None], runs(n1, H)] - s
    z = f64(gs) * (s * (sigmoid(st[np.arange(H)[:, None], runs(n2, H)])))
    h = 0.0625 * ((d_k1.T @ mxq(z, 0, "e4m3")))
    nw = h - h[:, unstriped(n5)]
    ph = np.zeros((H, U))
    ph[:, unstriped(n3)] = h
    out = ph.copy()
    out[:, unstriped(n4)] = nw
    return (out,) + planes(out)

@@ -1,0 +1,189 @@
+from contextlib import ExitStack
+
+import concourse.mybir as mybir
+
+K, T, S, G, H, U = 512, 1024, 256, 2048, 512, 512
+FLOPS = 2 * 2 * K * H * S
+
+F32 = mybir.dt.float32
+BF16 = mybir.dt.bfloat16
+U32 = mybir.dt.uint32
+I32 = mybir.dt.int32
+U16 = mybir.dt.uint16
+U8 = mybir.dt.uint8
+FP8X4 = mybir.dt.float8_e4m3fn_x4
+ACT = mybir.ActivationFunctionType
+ALU = mybir.AluOpType
+
+P = 128
+PACK = 4
+HALF = S // 2
+SIXTEENTH = 0.0625
+
+
+def tile_picked_hwqhopdpagq_none_po_kernel(
+    tc, x_words, x_scales, d_words, d_scales, gs, offs, ci, n1, n2, k1, n3, n4, n5, out_0, out_1, out_2
+):
+    nc = tc.nc
+    with ExitStack() as ctx:
+        lists = ctx.enter_context(tc.tile_pool(name="lists", bufs=1))
+        sb = ctx.enter_context(tc.tile_pool(name="sb", bufs=1))
+        psum = ctx.enter_context(tc.psum_pool(name="psum", bufs=1))
+
+        def load_list(name, dram):
+            held = lists.tile(list(dram.shape), U16, name=name)
+            nc.sync.dma_start(held[:], dram)
+            return held
+
+        def words_of(dram):
+            return dram[0].rearrange("p n t -> p (n t)").bitcast(I32)
+
+        def move_scale_rows(queue, placed, picked):
+            for r in range(4):
+                queue.dma_start(placed[r:P:32, :].bitcast(I32), picked[8 * r : P : 32, :].bitcast(I32))
+
+        x_byte_table = sb.tile([P, T], U8, name="x_byte_table", align_bytes=64)
+        d_byte_table = sb.tile([P, G], U8, name="d_byte_table", align_bytes=64)
+        x_word_table = sb.tile([P, T], U32, name="x_word_table", align_bytes=64)
+        d_word_table = sb.tile([P, G], U32, name="d_word_table", align_bytes=64)
+        offs_l = load_list("offs_l", offs)
+        ci_l = load_list("ci_l", ci)
+        nc.scalar.dma_start(x_byte_table[:].bitcast(I32), x_scales[0].bitcast(I32).unsqueeze(1).to_broadcast([16, 8, T // 4]))
+        nc.scalar.dma_start(d_byte_table[:].bitcast(I32), d_scales[0].bitcast(I32).unsqueeze(1).to_broadcast([16, 8, G // 4]))
+        k1_l = load_list("k1_l", k1)
+        n1_l = load_list("n1_l", n1)
+        n2_l = load_list("n2_l", n2)
+        nc.sync.dma_start(d_word_table[:].bitcast(I32), words_of(d_words))
+        nc.sync.dma_start(x_word_table[:].bitcast(I32), words_of(x_words))
+        n3_l = load_list("n3_l", n3)
+        n5_l = load_list("n5_l", n5)
+        n4_l = load_list("n4_l", n4)
+        gain = sb.tile([P, PACK], F32, name="gain")
+        nc.gpsimd.dma_start(gain[:], gs.rearrange("(p t) o -> p (t o)", t=PACK))
+
+        first_scales = sb.tile([P, S + H], U8, name="first_scales", align_bytes=64)
+        k1_scales = sb.tile([P, H], U8, name="k1_scales", align_bytes=64)
+        nc.vector.memset(first_scales[:].bitcast(I32), 0)
+        rows = [sb.tile([P, 2 * S], F32, name="rows%d" % t, align_bytes=64) for t in range(PACK)]
+        for t in range(PACK):
+            nc.vector.memset(rows[t][:, S:], 0.0)
+        nc.vector.memset(k1_scales[:].bitcast(I32), 0)
+
+        first_bytes = sb.tile([P, S + H], U8, name="first_bytes", align_bytes=64)
+        nc.vector.tensor_copy(first_bytes[:, :S], x_byte_table[:].indirect(offs_l[:]))
+        nc.vector.tensor_copy(
+            first_bytes[:, S:].rearrange("p (t m) -> p m t", t=PACK), d_byte_table[:].indirect(ci_l[:])
+        )
+        move_scale_rows(nc.scalar, first_scales, first_bytes)
+        ci_words = sb.tile([P, H], U32, name="ci_words", tag="picked_words", align_bytes=64)
+        nc.vector.tensor_copy(ci_words[:].rearrange("p (t m) -> p m t", t=PACK), d_word_table[:].indirect(ci_l[:]))
+        x_picked = sb.tile([P, S], U32, name="x_picked", tag="moving_then_dealt", align_bytes=64)
+        nc.vector.tensor_copy(x_picked[:], x_word_table[:].indirect(offs_l[:]))
+
+        for t in range(PACK):
+            acc = psum.tile([P, S], F32, name="s_acc%d" % t, tag="bank%d" % t)
+            nc.tensor.matmul_mx(
+                out=acc[:],
+                lhsT=ci_words[:, t * P : (t + 1) * P].bitcast(FP8X4),
+                lhsT_scale=first_scales[:, S + t * P : S + (t + 1) * P],
+                rhs=x_picked[:].bitcast(FP8X4),
+                rhs_scale=first_scales[:, :S],
+                start=True,
+                stop=True,
+            )
+            nc.vector.tensor_scalar_mul(rows[t][:, :S], acc[:], SIXTEENTH)
+
+        k1_bytes = sb.tile([P, H], U8, name="k1_bytes", align_bytes=64)
+        k1_bytes_dealt = sb.tile([P, H], U8, name="k1_bytes_dealt", tag="moving_then_dealt", align_bytes=64)
+        k1_picked = sb.tile([P, H], U32, name="k1_picked", tag="picked_words", align_bytes=64)
+        k1_words = sb.tile([P, H], U32, name="k1_words", align_bytes=64)
+
+        def pick_k1_bytes():
+            nc.vector.tensor_copy(k1_bytes[:], d_byte_table[:].indirect(k1_l[:]))
+            nc.vector.tensor_copy(
+                k1_bytes_dealt[:].rearrange("p (t m) -> p t m", t=PACK),
+                k1_bytes[:].rearrange("p (m t) -> p t m", t=PACK),
+            )
+            move_scale_rows(nc.sync, k1_scales, k1_bytes_dealt)
+
+        def pick_k1_words():
+            nc.vector.tensor_copy(k1_picked[:], d_word_table[:].indirect(k1_l[:]))
+            nc.vector.tensor_copy(
+                k1_words[:].rearrange("p (t m) -> p t m", t=PACK),
+                k1_picked[:].rearrange("p (m t) -> p t m", t=PACK),
+            )
+
+        diffs = [sb.tile([P, 2 * S], F32, name="diffs%d" % t, align_bytes=64) for t in range(PACK)]
+        pick_k1_bytes()
+        for t in range(PACK):
+            nc.scalar.activation(diffs[t][:, S:], rows[t][:].indirect(n1_l[:]), ACT.Copy)
+            nc.vector.tensor_tensor(diffs[t][:, :S], diffs[t][:, S:], rows[t][:, :S], ALU.subtract)
+        pick_k1_words()
+
+        pages = [sb.tile([P, U], F32, name="page%d" % t, align_bytes=64) for t in range(PACK)]
+        for half in range(2):
+            cols = slice(half * HALF, (half + 1) * HALF)
+            entries = slice(half * HALF // 16, (half + 1) * HALF // 16)
+            z_planes = sb.tile([P, PACK, HALF], BF16, name="z_planes%d" % half, align_bytes=64)
+            for t in range(PACK):
+                gate = sb.tile([P, HALF], F32, name="gate%d_%d" % (half, t), align_bytes=64)
+                nc.scalar.activation(gate[:], diffs[t][:].indirect(n2_l[:, entries]), ACT.Sigmoid)
+                nc.vector.scalar_tensor_tensor(
+                    z_planes[:, t, :], gate[:], gain[:, t : t + 1], rows[t][:, cols], ALU.mult, ALU.mult
+                )
+            z_grouped = sb.tile([P, HALF, PACK], BF16, name="z_grouped%d" % half, align_bytes=64)
+            nc.vector.tensor_copy(
+                z_grouped[:].rearrange("p (c i) t -> p c t i", i=4),
+                z_planes[:].rearrange("p t (c i) -> p c t i", i=4),
+            )
+            z_words = sb.tile([P, HALF], U32, name="z_words%d" % half, align_bytes=64)
+            z_scales = sb.tile([P, HALF], U8, name="z_scales%d" % half, align_bytes=64)
+            nc.vector.quantize_mx(
+                out=z_words[:].bitcast(FP8X4), scales=z_scales[:], in_=z_grouped[:].rearrange("p c t -> p (c t)")
+            )
+            for t in range(PACK):
+                bank = (PACK + t) if half == 0 else t
+                acc = psum.tile([P, HALF], F32, name="h_acc%d_%d" % (half, t), tag="bank%d" % bank)
+                nc.tensor.matmul_mx(
+                    out=acc[:],
+                    lhsT=k1_words[:, t * P : (t + 1) * P].bitcast(FP8X4),
+                    lhsT_scale=k1_scales[:, t * P : (t + 1) * P],
+                    rhs=z_words[:].bitcast(FP8X4),
+                    rhs_scale=z_scales[:],
+                    start=True,
+                    stop=True,
+                )
+                nc.vector.tensor_scalar_mul(rows[t][:, cols], acc[:], SIXTEENTH)
+
+        for t in range(PACK):
+            nc.scalar.activation(pages[t][:].indirect(n3_l[:, : HALF // 16]), rows[t][:, :HALF], ACT.Copy)
+
+        out_rows = out_0.rearrange("(p t) w -> p t w", t=PACK)
+        page_grouped = sb.tile([P, U, PACK], BF16, name="page_grouped", align_bytes=64)
+        for t in range(PACK):
+            fetched = sb.tile([P, S], F32, name="fetched%d" % t, align_bytes=64)
+            nw = sb.tile([P, S], F32, name="nw%d" % t, align_bytes=64)
+            nc.scalar.activation(fetched[:], rows[t][:].indirect(n5_l[:]), ACT.Copy)
+            nc.vector.tensor_tensor(nw[:], rows[t][:, :S], fetched[:], ALU.subtract)
+            nc.scalar.activation(pages[t][:].indirect(n3_l[:, HALF // 16 :]), rows[t][:, HALF:S], ACT.Copy)
+            nc.scalar.activation(pages[t][:].indirect(n4_l[:]), nw[:], ACT.Copy)
+            nc.sync.dma_start(out_rows[:, t, :], pages[t][:])
+            for half in range(2):
+                slots = slice(half * U // 2, (half + 1) * U // 2)
+                nc.vector.tensor_copy(page_grouped[:, slots, t], pages[t][:, slots])
+
+        page_words = sb.tile([P, U], U32, name="page_words", align_bytes=64)
+        page_scales = sb.tile([P, U], U8, name="page_scales", align_bytes=64)
+        for half in range(2):
+            slots = slice(half * U // 2, (half + 1) * U // 2)
+            nc.vector.quantize_mx(
+                out=page_words[:, slots].bitcast(FP8X4),
+                scales=page_scales[:, slots],
+                in_=page_grouped[:, slots, :].rearrange("p c t -> p (c t)"),
+            )
+            nc.sync.dma_start(words_of(out_1)[:, slots], page_words[:, slots].bitcast(I32))
+        for q in range(4):
+            queue = nc.scalar if q % 2 == 0 else nc.sync
+            queue.dma_start(
+                out_2[0][4 * q : 4 * q + 4, :].bitcast(I32), page_scales[32 * q : 32 * q + 4, :].bitcast(I32)
+            )

@@ -42,6 +42,11 @@ def tile_picked_hwqhopdpagq_none_po_kernel(
             for r in range(4):
                 queue.dma_start(placed[r:P:32, :].bitcast(I32), picked[8 * r : P : 32, :].bitcast(I32))
 
+        warm_in = sb.tile([P, 1], F32, name="warm_in")
+        warm_out = sb.tile([P, 1], F32, name="warm_out")
+        nc.vector.memset(warm_in[:], 0.0)
+        nc.scalar.activation(warm_out[:], warm_in[:], ACT.Sigmoid)
+
         x_byte_table = sb.tile([P, T], U8, name="x_byte_table", align_bytes=64)
         d_byte_table = sb.tile([P, G], U8, name="d_byte_table", align_bytes=64)
         x_word_table = sb.tile([P, T], U32, name="x_word_table", align_bytes=64)

@@ -49,7 +49,7 @@ def tile_picked_hwqhopdpagq_none_po_kernel(
 
         x_byte_table = sb.tile([P, T], U8, name="x_byte_table", align_bytes=64)
         d_byte_table = sb.tile([P, G], U8, name="d_byte_table", align_bytes=64)
-        x_word_table = sb.tile([P, T], U32, name="x_word_table", align_bytes=64)
+        x_word_table = sb.tile([P, T], U32, name="x_word_table", tag="slot_x_table", align_bytes=64)
         d_word_table = sb.tile([P, G], U32, name="d_word_table", align_bytes=64)
         offs_l = load_list("offs_l", offs)
         ci_l = load_list("ci_l", ci)
@@ -74,7 +74,7 @@ def tile_picked_hwqhopdpagq_none_po_kernel(
             nc.vector.memset(rows[t][:, S:], 0.0)
         nc.vector.memset(k1_scales[:].bitcast(I32), 0)
 
-        first_bytes = sb.tile([P, S + H], U8, name="first_bytes", align_bytes=64)
+        first_bytes = sb.tile([P, S + H], U8, name="first_bytes", tag="slot_first_bytes", align_bytes=64)
         nc.vector.tensor_copy(first_bytes[:, :S], x_byte_table[:].indirect(offs_l[:]))
         nc.vector.tensor_copy(
             first_bytes[:, S:].rearrange("p (t m) -> p m t", t=PACK), d_byte_table[:].indirect(ci_l[:])
@@ -98,54 +98,65 @@ def tile_picked_hwqhopdpagq_none_po_kernel(
             )
             nc.vector.tensor_scalar_mul(rows[t][:, :S], acc[:], SIXTEENTH)
 
-        k1_bytes = sb.tile([P, H], U8, name="k1_bytes", align_bytes=64)
-        k1_bytes_dealt = sb.tile([P, H], U8, name="k1_bytes_dealt", tag="moving_then_dealt", align_bytes=64)
-        k1_picked = sb.tile([P, H], U32, name="k1_picked", tag="picked_words", align_bytes=64)
-        k1_words = sb.tile([P, H], U32, name="k1_words", align_bytes=64)
-
-        def pick_k1_bytes():
-            nc.vector.tensor_copy(k1_bytes[:], d_byte_table[:].indirect(k1_l[:]))
+        k1_half = H // 2
+        byte_tags = ["slot_k1_bytes", "moving_then_dealt"]
+        word_tags = ["slot_x_table", "picked_words"]
+        k1_bytes_dealt = sb.tile([P, H], U8, name="k1_bytes_dealt", tag="slot_first_bytes", align_bytes=64)
+        k1_picked = []
+        for half in range(2):
+            entries = slice(half * k1_half // 16, (half + 1) * k1_half // 16)
+            k1_bytes = sb.tile([P, k1_half], U8, name="k1_bytes%d" % half, tag=byte_tags[half], align_bytes=64)
+            nc.vector.tensor_copy(k1_bytes[:], d_byte_table[:].indirect(k1_l[:, entries]))
             nc.vector.tensor_copy(
-                k1_bytes_dealt[:].rearrange("p (t m) -> p t m", t=PACK),
+                k1_bytes_dealt[:].rearrange("p (t u m) -> p u t m", t=PACK, u=2)[:, half],
                 k1_bytes[:].rearrange("p (m t) -> p t m", t=PACK),
             )
-            move_scale_rows(nc.sync, k1_scales, k1_bytes_dealt)
-
-        def pick_k1_words():
-            nc.vector.tensor_copy(k1_picked[:], d_word_table[:].indirect(k1_l[:]))
-            nc.vector.tensor_copy(
-                k1_words[:].rearrange("p (t m) -> p t m", t=PACK),
-                k1_picked[:].rearrange("p (m t) -> p t m", t=PACK),
-            )
+            picked = sb.tile([P, k1_half], U32, name="k1_picked%d" % half, tag=word_tags[half], align_bytes=64)
+            nc.vector.tensor_copy(picked[:], d_word_table[:].indirect(k1_l[:, entries]))
+            k1_picked.append(picked)
+        move_scale_rows(nc.sync, k1_scales, k1_bytes_dealt)
 
         diffs = [sb.tile([P, 2 * S], F32, name="diffs%d" % t, align_bytes=64) for t in range(PACK)]
-        pick_k1_bytes()
         for t in range(PACK):
             nc.scalar.activation(diffs[t][:, S:], rows[t][:].indirect(n1_l[:]), ACT.Copy)
             nc.vector.tensor_tensor(diffs[t][:, :S], diffs[t][:, S:], rows[t][:, :S], ALU.subtract)
-        pick_k1_words()
 
         pages = [sb.tile([P, U], F32, name="page%d" % t, align_bytes=64) for t in range(PACK)]
+        gate_tags = [["gate0", "gate1", "gate2", "gate3"], ["gate0", "gate2", "gate3", "picked_words"]]
         for half in range(2):
             cols = slice(half * HALF, (half + 1) * HALF)
             entries = slice(half * HALF // 16, (half + 1) * HALF // 16)
-            z_planes = sb.tile([P, PACK, HALF], BF16, name="z_planes%d" % half, align_bytes=64)
+            z_planes = sb.tile([P, PACK - 1, HALF], BF16, name="z_planes%d" % half, tag=["slot_z_planes", "slot_z_grouped"][half], align_bytes=64)
+            z_grouped = sb.tile([P, HALF, PACK], BF16, name="z_grouped%d" % half, tag=["slot_z_grouped", "slot_z_words"][half], align_bytes=64)
             for t in range(PACK):
-                gate = sb.tile([P, HALF], F32, name="gate%d_%d" % (half, t), align_bytes=64)
+                gate = sb.tile([P, HALF], F32, name="gate%d_%d" % (half, t), tag=gate_tags[half][t], align_bytes=64)
                 nc.scalar.activation(gate[:], diffs[t][:].indirect(n2_l[:, entries]), ACT.Sigmoid)
+                last = t == PACK - 1
+                if last:
+                    nc.vector.tensor_copy(
+                        z_grouped[:, :, :t].rearrange("p (c i) t -> p c t i", i=4),
+                        z_planes[:].rearrange("p t (c i) -> p c t i", i=4),
+                    )
                 nc.vector.scalar_tensor_tensor(
-                    z_planes[:, t, :], gate[:], gain[:, t : t + 1], rows[t][:, cols], ALU.mult, ALU.mult
+                    z_grouped[:, :, t] if last else z_planes[:, t, :],
+                    gate[:],
+                    gain[:, t : t + 1],
+                    rows[t][:, cols],
+                    ALU.mult,
+                    ALU.mult,
                 )
-            z_grouped = sb.tile([P, HALF, PACK], BF16, name="z_grouped%d" % half, align_bytes=64)
-            nc.vector.tensor_copy(
-                z_grouped[:].rearrange("p (c i) t -> p c t i", i=4),
-                z_planes[:].rearrange("p t (c i) -> p c t i", i=4),
-            )
-            z_words = sb.tile([P, HALF], U32, name="z_words%d" % half, align_bytes=64)
+            z_words = sb.tile([P, HALF], U32, name="z_words%d" % half, tag=["slot_z_words", "slot_z_planes"][half], align_bytes=64)
             z_scales = sb.tile([P, HALF], U8, name="z_scales%d" % half, align_bytes=64)
             nc.vector.quantize_mx(
                 out=z_words[:].bitcast(FP8X4), scales=z_scales[:], in_=z_grouped[:].rearrange("p c t -> p (c t)")
             )
+            if half == 0:
+                k1_words = sb.tile([P, H], U32, name="k1_words", tag="gate1", align_bytes=64)
+                for piece in range(2):
+                    nc.vector.tensor_copy(
+                        k1_words[:].rearrange("p (t u m) -> p u t m", t=PACK, u=2)[:, piece],
+                        k1_picked[piece][:].rearrange("p (m t) -> p t m", t=PACK),
+                    )
             for t in range(PACK):
                 bank = (PACK + t) if half == 0 else t
                 acc = psum.tile([P, HALF], F32, name="h_acc%d_%d" % (half, t), tag="bank%d" % bank)

@@ -17,6 +17,10 @@ ALU = mybir.AluOpType
 
 P = 128
 PACK = 4
+BLOCKS = 16
+BLOCK_PARTITIONS = 8
+QUADRANT = 32
+COLUMN_ENTRIES = 16
 HALF = S // 2
 SIXTEENTH = 0.0625
 
@@ -35,12 +39,23 @@ def tile_picked_hwqhopdpagq_none_po_kernel(
             nc.sync.dma_start(held[:], dram)
             return held
 
+        def list_columns(first, end):
+            return slice(first // COLUMN_ENTRIES, end // COLUMN_ENTRIES)
+
         def words_of(dram):
             return dram[0].rearrange("p n t -> p (n t)").bitcast(I32)
 
+        def load_scale_rows(table, dram):
+            rows_as_words = dram[0].bitcast(I32)
+            spread = rows_as_words.unsqueeze(1).to_broadcast([BLOCKS, BLOCK_PARTITIONS, rows_as_words.shape[1]])
+            nc.scalar.dma_start(table[:].bitcast(I32), spread)
+
         def move_scale_rows(queue, placed, picked):
-            for r in range(4):
-                queue.dma_start(placed[r:P:32, :].bitcast(I32), picked[8 * r : P : 32, :].bitcast(I32))
+            for r in range(QUADRANT // BLOCK_PARTITIONS):
+                queue.dma_start(
+                    placed[r:P:QUADRANT, :].bitcast(I32),
+                    picked[BLOCK_PARTITIONS * r : P : QUADRANT, :].bitcast(I32),
+                )
 
         warm_in = sb.tile([P, 1], F32, name="warm_in")
         warm_out = sb.tile([P, 1], F32, name="warm_out")
@@ -53,8 +68,8 @@ def tile_picked_hwqhopdpagq_none_po_kernel(
         d_word_table = sb.tile([P, G], U32, name="d_word_table", align_bytes=64)
         offs_l = load_list("offs_l", offs)
         ci_l = load_list("ci_l", ci)
-        nc.scalar.dma_start(x_byte_table[:].bitcast(I32), x_scales[0].bitcast(I32).unsqueeze(1).to_broadcast([16, 8, T // 4]))
-        nc.scalar.dma_start(d_byte_table[:].bitcast(I32), d_scales[0].bitcast(I32).unsqueeze(1).to_broadcast([16, 8, G // 4]))
+        load_scale_rows(x_byte_table, x_scales)
+        load_scale_rows(d_byte_table, d_scales)
         k1_l = load_list("k1_l", k1)
         n1_l = load_list("n1_l", n1)
         n2_l = load_list("n2_l", n2)
@@ -98,20 +113,20 @@ def tile_picked_hwqhopdpagq_none_po_kernel(
             )
             nc.vector.tensor_scalar_mul(rows[t][:, :S], acc[:], SIXTEENTH)
 
-        k1_half = H // 2
+        piece_entries = H // 2
         byte_tags = ["slot_k1_bytes", "moving_then_dealt"]
         word_tags = ["slot_x_table", "picked_words"]
         k1_bytes_dealt = sb.tile([P, H], U8, name="k1_bytes_dealt", tag="slot_first_bytes", align_bytes=64)
         k1_picked = []
-        for half in range(2):
-            entries = slice(half * k1_half // 16, (half + 1) * k1_half // 16)
-            k1_bytes = sb.tile([P, k1_half], U8, name="k1_bytes%d" % half, tag=byte_tags[half], align_bytes=64)
+        for piece in range(2):
+            entries = list_columns(piece * piece_entries, (piece + 1) * piece_entries)
+            k1_bytes = sb.tile([P, piece_entries], U8, name="k1_bytes%d" % piece, tag=byte_tags[piece], align_bytes=64)
             nc.vector.tensor_copy(k1_bytes[:], d_byte_table[:].indirect(k1_l[:, entries]))
             nc.vector.tensor_copy(
-                k1_bytes_dealt[:].rearrange("p (t u m) -> p u t m", t=PACK, u=2)[:, half],
+                k1_bytes_dealt[:].rearrange("p (t u m) -> p u t m", t=PACK, u=2)[:, piece],
                 k1_bytes[:].rearrange("p (m t) -> p t m", t=PACK),
             )
-            picked = sb.tile([P, k1_half], U32, name="k1_picked%d" % half, tag=word_tags[half], align_bytes=64)
+            picked = sb.tile([P, piece_entries], U32, name="k1_picked%d" % piece, tag=word_tags[piece], align_bytes=64)
             nc.vector.tensor_copy(picked[:], d_word_table[:].indirect(k1_l[:, entries]))
             k1_picked.append(picked)
         move_scale_rows(nc.sync, k1_scales, k1_bytes_dealt)
@@ -123,11 +138,16 @@ def tile_picked_hwqhopdpagq_none_po_kernel(
 
         pages = [sb.tile([P, U], F32, name="page%d" % t, align_bytes=64) for t in range(PACK)]
         gate_tags = [["gate0", "gate1", "gate2", "gate3"], ["gate0", "gate2", "gate3", "picked_words"]]
+        planes_tags = ["slot_z_planes", "slot_z_grouped"]
+        grouped_tags = ["slot_z_grouped", "slot_z_words"]
+        words_tags = ["slot_z_words", "slot_z_planes"]
         for half in range(2):
-            cols = slice(half * HALF, (half + 1) * HALF)
-            entries = slice(half * HALF // 16, (half + 1) * HALF // 16)
-            z_planes = sb.tile([P, PACK - 1, HALF], BF16, name="z_planes%d" % half, tag=["slot_z_planes", "slot_z_grouped"][half], align_bytes=64)
-            z_grouped = sb.tile([P, HALF, PACK], BF16, name="z_grouped%d" % half, tag=["slot_z_grouped", "slot_z_words"][half], align_bytes=64)
+            places = slice(half * HALF, (half + 1) * HALF)
+            entries = list_columns(places.start, places.stop)
+            z_planes = sb.tile(
+                [P, PACK - 1, HALF], BF16, name="z_planes%d" % half, tag=planes_tags[half], align_bytes=64
+            )
+            z_grouped = sb.tile([P, HALF, PACK], BF16, name="z_grouped%d" % half, tag=grouped_tags[half], align_bytes=64)
             for t in range(PACK):
                 gate = sb.tile([P, HALF], F32, name="gate%d_%d" % (half, t), tag=gate_tags[half][t], align_bytes=64)
                 nc.scalar.activation(gate[:], diffs[t][:].indirect(n2_l[:, entries]), ACT.Sigmoid)
@@ -141,11 +161,11 @@ def tile_picked_hwqhopdpagq_none_po_kernel(
                     z_grouped[:, :, t] if last else z_planes[:, t, :],
                     gate[:],
                     gain[:, t : t + 1],
-                    rows[t][:, cols],
+                    rows[t][:, places],
                     ALU.mult,
                     ALU.mult,
                 )
-            z_words = sb.tile([P, HALF], U32, name="z_words%d" % half, tag=["slot_z_words", "slot_z_planes"][half], align_bytes=64)
+            z_words = sb.tile([P, HALF], U32, name="z_words%d" % half, tag=words_tags[half], align_bytes=64)
             z_scales = sb.tile([P, HALF], U8, name="z_scales%d" % half, align_bytes=64)
             nc.vector.quantize_mx(
                 out=z_words[:].bitcast(FP8X4), scales=z_scales[:], in_=z_grouped[:].rearrange("p c t -> p (c t)")
@@ -169,37 +189,52 @@ def tile_picked_hwqhopdpagq_none_po_kernel(
                     start=True,
                     stop=True,
                 )
-                nc.vector.tensor_scalar_mul(rows[t][:, cols], acc[:], SIXTEENTH)
+                nc.vector.tensor_scalar_mul(rows[t][:, places], acc[:], SIXTEENTH)
 
         for t in range(PACK):
-            nc.scalar.activation(pages[t][:].indirect(n3_l[:, : HALF // 16]), rows[t][:, :HALF], ACT.Copy)
+            nc.scalar.activation(pages[t][:].indirect(n3_l[:, list_columns(0, HALF)]), rows[t][:, :HALF], ACT.Copy)
 
         out_rows = out_0.rearrange("(p t) w -> p t w", t=PACK)
-        page_grouped = sb.tile([P, U, PACK], BF16, name="page_grouped", align_bytes=64)
-        for t in range(PACK):
+        half_page = U // 2
+        page_grouped = [sb.tile([P, half_page, PACK], BF16, name="page_grouped%d" % u, align_bytes=64) for u in range(2)]
+        order = [2, 0, 1, 3]
+        nw = {}
+
+        def fetch_and_subtract(t):
             fetched = sb.tile([P, S], F32, name="fetched%d" % t, align_bytes=64)
-            nw = sb.tile([P, S], F32, name="nw%d" % t, align_bytes=64)
+            nw[t] = sb.tile([P, S], F32, name="nw%d" % t, align_bytes=64)
             nc.scalar.activation(fetched[:], rows[t][:].indirect(n5_l[:]), ACT.Copy)
-            nc.vector.tensor_tensor(nw[:], rows[t][:, :S], fetched[:], ALU.subtract)
-            nc.scalar.activation(pages[t][:].indirect(n3_l[:, HALF // 16 :]), rows[t][:, HALF:S], ACT.Copy)
-            nc.scalar.activation(pages[t][:].indirect(n4_l[:]), nw[:], ACT.Copy)
+            nc.vector.tensor_tensor(nw[t][:], rows[t][:, :S], fetched[:], ALU.subtract)
+
+        fetch_and_subtract(order[0])
+        for step, t in enumerate(order):
+            more = step + 1 < PACK
+            nc.scalar.activation(pages[t][:].indirect(n3_l[:, list_columns(HALF, S)]), rows[t][:, HALF:S], ACT.Copy)
+            if more:
+                fetch_and_subtract(order[step + 1])
+            nc.scalar.activation(pages[t][:].indirect(n4_l[:]), nw[t][:], ACT.Copy)
             nc.sync.dma_start(out_rows[:, t, :], pages[t][:])
-            for half in range(2):
-                slots = slice(half * U // 2, (half + 1) * U // 2)
-                nc.vector.tensor_copy(page_grouped[:, slots, t], pages[t][:, slots])
+            nc.vector.tensor_copy(page_grouped[0][:, :, t], pages[t][:, :half_page])
+            if more:
+                nc.vector.tensor_copy(page_grouped[1][:, :, t], pages[t][:, half_page:])
+            else:
+                quarter = half_page // 2
+                nc.vector.tensor_copy(page_grouped[1][:, :quarter, t], pages[t][:, half_page : half_page + quarter])
+                nc.scalar.copy(page_grouped[1][:, quarter:, t], pages[t][:, half_page + quarter :])
 
         page_words = sb.tile([P, U], U32, name="page_words", align_bytes=64)
         page_scales = sb.tile([P, U], U8, name="page_scales", align_bytes=64)
-        for half in range(2):
-            slots = slice(half * U // 2, (half + 1) * U // 2)
+        for u in range(2):
+            columns = slice(u * half_page, (u + 1) * half_page)
             nc.vector.quantize_mx(
-                out=page_words[:, slots].bitcast(FP8X4),
-                scales=page_scales[:, slots],
-                in_=page_grouped[:, slots, :].rearrange("p c t -> p (c t)"),
+                out=page_words[:, columns].bitcast(FP8X4),
+                scales=page_scales[:, columns],
+                in_=page_grouped[u][:].rearrange("p c t -> p (c t)"),
             )
-            nc.sync.dma_start(words_of(out_1)[:, slots], page_words[:, slots].bitcast(I32))
-        for q in range(4):
+            nc.sync.dma_start(words_of(out_1)[:, columns], page_words[:, columns].bitcast(I32))
+        for q in range(P // QUADRANT):
             queue = nc.scalar if q % 2 == 0 else nc.sync
             queue.dma_start(
-                out_2[0][4 * q : 4 * q + 4, :].bitcast(I32), page_scales[32 * q : 32 * q + 4, :].bitcast(I32)
+                out_2[0][4 * q : 4 * q + 4, :].bitcast(I32),
+                page_scales[QUADRANT * q : QUADRANT * q + 4, :].bitcast(I32),
             )

from contextlib import ExitStack

import concourse.mybir as mybir

K, T, S, G, H, U = 512, 1024, 256, 2048, 512, 512
FLOPS = 2 * 2 * K * H * S

F32 = mybir.dt.float32
BF16 = mybir.dt.bfloat16
U32 = mybir.dt.uint32
I32 = mybir.dt.int32
U16 = mybir.dt.uint16
U8 = mybir.dt.uint8
FP8X4 = mybir.dt.float8_e4m3fn_x4
ACT = mybir.ActivationFunctionType
ALU = mybir.AluOpType

P = 128
PACK = 4
BLOCKS = 16
BLOCK_PARTITIONS = 8
QUADRANT = 32
COLUMN_ENTRIES = 16
HALF = S // 2
SIXTEENTH = 0.0625


def tile_picked_hwqhopdpagq_none_po_kernel(
    tc, x_words, x_scales, d_words, d_scales, gs, offs, ci, n1, n2, k1, n3, n4, n5, out_0, out_1, out_2
):
    nc = tc.nc
    with ExitStack() as ctx:
        lists = ctx.enter_context(tc.tile_pool(name="lists", bufs=1))
        sb = ctx.enter_context(tc.tile_pool(name="sb", bufs=1))
        psum = ctx.enter_context(tc.psum_pool(name="psum", bufs=1))

        def load_list(name, dram):
            held = lists.tile(list(dram.shape), U16, name=name)
            nc.sync.dma_start(held[:], dram)
            return held

        def list_columns(first, end):
            return slice(first // COLUMN_ENTRIES, end // COLUMN_ENTRIES)

        def words_of(dram):
            return dram[0].rearrange("p n t -> p (n t)").bitcast(I32)

        def load_scale_rows(table, dram):
            rows_as_words = dram[0].bitcast(I32)
            spread = rows_as_words.unsqueeze(1).to_broadcast([BLOCKS, BLOCK_PARTITIONS, rows_as_words.shape[1]])
            nc.scalar.dma_start(table[:].bitcast(I32), spread)

        def move_scale_rows(queue, placed, picked):
            for r in range(QUADRANT // BLOCK_PARTITIONS):
                queue.dma_start(
                    placed[r:P:QUADRANT, :].bitcast(I32),
                    picked[BLOCK_PARTITIONS * r : P : QUADRANT, :].bitcast(I32),
                )

        warm_in = sb.tile([P, 1], F32, name="warm_in")
        warm_out = sb.tile([P, 1], F32, name="warm_out")
        nc.vector.memset(warm_in[:], 0.0)
        nc.scalar.activation(warm_out[:], warm_in[:], ACT.Sigmoid)

        x_byte_table = sb.tile([P, T], U8, name="x_byte_table", align_bytes=64)
        d_byte_table = sb.tile([P, G], U8, name="d_byte_table", align_bytes=64)
        x_word_table = sb.tile([P, T], U32, name="x_word_table", tag="slot_x_table", align_bytes=64)
        d_word_table = sb.tile([P, G], U32, name="d_word_table", align_bytes=64)
        offs_l = load_list("offs_l", offs)
        ci_l = load_list("ci_l", ci)
        load_scale_rows(x_byte_table, x_scales)
        load_scale_rows(d_byte_table, d_scales)
        k1_l = load_list("k1_l", k1)
        n1_l = load_list("n1_l", n1)
        n2_l = load_list("n2_l", n2)
        nc.sync.dma_start(d_word_table[:].bitcast(I32), words_of(d_words))
        nc.sync.dma_start(x_word_table[:].bitcast(I32), words_of(x_words))
        n3_l = load_list("n3_l", n3)
        n5_l = load_list("n5_l", n5)
        n4_l = load_list("n4_l", n4)
        gain = sb.tile([P, PACK], F32, name="gain")
        nc.gpsimd.dma_start(gain[:], gs.rearrange("(p t) o -> p (t o)", t=PACK))

        first_scales = sb.tile([P, S + H], U8, name="first_scales", align_bytes=64)
        k1_scales = sb.tile([P, H], U8, name="k1_scales", align_bytes=64)
        nc.vector.memset(first_scales[:].bitcast(I32), 0)
        rows = [sb.tile([P, 2 * S], F32, name="rows%d" % t, align_bytes=64) for t in range(PACK)]
        for t in range(PACK):
            nc.vector.memset(rows[t][:, S:], 0.0)
        nc.vector.memset(k1_scales[:].bitcast(I32), 0)

        first_bytes = sb.tile([P, S + H], U8, name="first_bytes", tag="slot_first_bytes", align_bytes=64)
        nc.vector.tensor_copy(first_bytes[:, :S], x_byte_table[:].indirect(offs_l[:]))
        nc.vector.tensor_copy(
            first_bytes[:, S:].rearrange("p (t m) -> p m t", t=PACK), d_byte_table[:].indirect(ci_l[:])
        )
        move_scale_rows(nc.scalar, first_scales, first_bytes)
        ci_words = sb.tile([P, H], U32, name="ci_words", tag="picked_words", align_bytes=64)
        nc.vector.tensor_copy(ci_words[:].rearrange("p (t m) -> p m t", t=PACK), d_word_table[:].indirect(ci_l[:]))
        x_picked = sb.tile([P, S], U32, name="x_picked", tag="moving_then_dealt", align_bytes=64)
        nc.vector.tensor_copy(x_picked[:], x_word_table[:].indirect(offs_l[:]))

        for t in range(PACK):
            acc = psum.tile([P, S], F32, name="s_acc%d" % t, tag="bank%d" % t)
            nc.tensor.matmul_mx(
                out=acc[:],
                lhsT=ci_words[:, t * P : (t + 1) * P].bitcast(FP8X4),
                lhsT_scale=first_scales[:, S + t * P : S + (t + 1) * P],
                rhs=x_picked[:].bitcast(FP8X4),
                rhs_scale=first_scales[:, :S],
                start=True,
                stop=True,
            )
            nc.vector.tensor_scalar_mul(rows[t][:, :S], acc[:], SIXTEENTH)

        piece_entries = H // 2
        byte_tags = ["slot_k1_bytes", "moving_then_dealt"]
        word_tags = ["slot_x_table", "picked_words"]
        k1_bytes_dealt = sb.tile([P, H], U8, name="k1_bytes_dealt", tag="slot_first_bytes", align_bytes=64)
        k1_picked = []
        for piece in range(2):
            entries = list_columns(piece * piece_entries, (piece + 1) * piece_entries)
            k1_bytes = sb.tile([P, piece_entries], U8, name="k1_bytes%d" % piece, tag=byte_tags[piece], align_bytes=64)
            nc.vector.tensor_copy(k1_bytes[:], d_byte_table[:].indirect(k1_l[:, entries]))
            nc.vector.tensor_copy(
                k1_bytes_dealt[:].rearrange("p (t u m) -> p u t m", t=PACK, u=2)[:, piece],
                k1_bytes[:].rearrange("p (m t) -> p t m", t=PACK),
            )
            picked = sb.tile([P, piece_entries], U32, name="k1_picked%d" % piece, tag=word_tags[piece], align_bytes=64)
            nc.vector.tensor_copy(picked[:], d_word_table[:].indirect(k1_l[:, entries]))
            k1_picked.append(picked)
        move_scale_rows(nc.sync, k1_scales, k1_bytes_dealt)

        diffs = [sb.tile([P, 2 * S], F32, name="diffs%d" % t, align_bytes=64) for t in range(PACK)]
        for t in range(PACK):
            nc.scalar.activation(diffs[t][:, S:], rows[t][:].indirect(n1_l[:]), ACT.Copy)
            nc.vector.tensor_tensor(diffs[t][:, :S], diffs[t][:, S:], rows[t][:, :S], ALU.subtract)

        pages = [sb.tile([P, U], F32, name="page%d" % t, align_bytes=64) for t in range(PACK)]
        gate_tags = [["gate0", "gate1", "gate2", "gate3"], ["gate0", "gate2", "gate3", "picked_words"]]
        planes_tags = ["slot_z_planes", "slot_z_grouped"]
        grouped_tags = ["slot_z_grouped", "slot_z_words"]
        words_tags = ["slot_z_words", "slot_z_planes"]
        for half in range(2):
            places = slice(half * HALF, (half + 1) * HALF)
            entries = list_columns(places.start, places.stop)
            z_planes = sb.tile(
                [P, PACK - 1, HALF], BF16, name="z_planes%d" % half, tag=planes_tags[half], align_bytes=64
            )
            z_grouped = sb.tile([P, HALF, PACK], BF16, name="z_grouped%d" % half, tag=grouped_tags[half], align_bytes=64)
            for t in range(PACK):
                gate = sb.tile([P, HALF], F32, name="gate%d_%d" % (half, t), tag=gate_tags[half][t], align_bytes=64)
                nc.scalar.activation(gate[:], diffs[t][:].indirect(n2_l[:, entries]), ACT.Sigmoid)
                last = t == PACK - 1
                if last:
                    nc.vector.tensor_copy(
                        z_grouped[:, :, :t].rearrange("p (c i) t -> p c t i", i=4),
                        z_planes[:].rearrange("p t (c i) -> p c t i", i=4),
                    )
                nc.vector.scalar_tensor_tensor(
                    z_grouped[:, :, t] if last else z_planes[:, t, :],
                    gate[:],
                    gain[:, t : t + 1],
                    rows[t][:, places],
                    ALU.mult,
                    ALU.mult,
                )
            z_words = sb.tile([P, HALF], U32, name="z_words%d" % half, tag=words_tags[half], align_bytes=64)
            z_scales = sb.tile([P, HALF], U8, name="z_scales%d" % half, align_bytes=64)
            nc.vector.quantize_mx(
                out=z_words[:].bitcast(FP8X4), scales=z_scales[:], in_=z_grouped[:].rearrange("p c t -> p (c t)")
            )
            if half == 0:
                k1_words = sb.tile([P, H], U32, name="k1_words", tag="gate1", align_bytes=64)
                for piece in range(2):
                    nc.vector.tensor_copy(
                        k1_words[:].rearrange("p (t u m) -> p u t m", t=PACK, u=2)[:, piece],
                        k1_picked[piece][:].rearrange("p (m t) -> p t m", t=PACK),
                    )
            for t in range(PACK):
                bank = (PACK + t) if half == 0 else t
                acc = psum.tile([P, HALF], F32, name="h_acc%d_%d" % (half, t), tag="bank%d" % bank)
                nc.tensor.matmul_mx(
                    out=acc[:],
                    lhsT=k1_words[:, t * P : (t + 1) * P].bitcast(FP8X4),
                    lhsT_scale=k1_scales[:, t * P : (t + 1) * P],
                    rhs=z_words[:].bitcast(FP8X4),
                    rhs_scale=z_scales[:],
                    start=True,
                    stop=True,
                )
                nc.vector.tensor_scalar_mul(rows[t][:, places], acc[:], SIXTEENTH)

        for t in range(PACK):
            nc.scalar.activation(pages[t][:].indirect(n3_l[:, list_columns(0, HALF)]), rows[t][:, :HALF], ACT.Copy)

        out_rows = out_0.rearrange("(p t) w -> p t w", t=PACK)
        half_page = U // 2
        page_grouped = [sb.tile([P, half_page, PACK], BF16, name="page_grouped%d" % u, align_bytes=64) for u in range(2)]
        order = [2, 0, 1, 3]
        nw = {}

        def fetch_and_subtract(t):
            fetched = sb.tile([P, S], F32, name="fetched%d" % t, align_bytes=64)
            nw[t] = sb.tile([P, S], F32, name="nw%d" % t, align_bytes=64)
            nc.scalar.activation(fetched[:], rows[t][:].indirect(n5_l[:]), ACT.Copy)
            nc.vector.tensor_tensor(nw[t][:], rows[t][:, :S], fetched[:], ALU.subtract)

        fetch_and_subtract(order[0])
        for step, t in enumerate(order):
            more = step + 1 < PACK
            nc.scalar.activation(pages[t][:].indirect(n3_l[:, list_columns(HALF, S)]), rows[t][:, HALF:S], ACT.Copy)
            if more:
                fetch_and_subtract(order[step + 1])
            nc.scalar.activation(pages[t][:].indirect(n4_l[:]), nw[t][:], ACT.Copy)
            nc.sync.dma_start(out_rows[:, t, :], pages[t][:])
            nc.vector.tensor_copy(page_grouped[0][:, :, t], pages[t][:, :half_page])
            if more:
                nc.vector.tensor_copy(page_grouped[1][:, :, t], pages[t][:, half_page:])
            else:
                quarter = half_page // 2
                nc.vector.tensor_copy(page_grouped[1][:, :quarter, t], pages[t][:, half_page : half_page + quarter])
                nc.scalar.copy(page_grouped[1][:, quarter:, t], pages[t][:, half_page + quarter :])

        page_words = sb.tile([P, U], U32, name="page_words", align_bytes=64)
        page_scales = sb.tile([P, U], U8, name="page_scales", align_bytes=64)
        for u in range(2):
            columns = slice(u * half_page, (u + 1) * half_page)
            nc.vector.quantize_mx(
                out=page_words[:, columns].bitcast(FP8X4),
                scales=page_scales[:, columns],
                in_=page_grouped[u][:].rearrange("p c t -> p (c t)"),
            )
            nc.sync.dma_start(words_of(out_1)[:, columns], page_words[:, columns].bitcast(I32))
        for q in range(P // QUADRANT):
            queue = nc.scalar if q % 2 == 0 else nc.sync
            queue.dma_start(
                out_2[0][4 * q : 4 * q + 4, :].bitcast(I32),
                page_scales[QUADRANT * q : QUADRANT * q + 4, :].bitcast(I32),
            )
